import numpy as np
import ml_dtypes


def mxq(x, axis, fmt="e4m3"):
    dtype, down = {"e4m3": (ml_dtypes.float8_e4m3fn, 7), "e5m2": (ml_dtypes.float8_e5m2, 14)}[fmt]
    v = np.moveaxis(np.asarray(x, np.float32).astype(ml_dtypes.bfloat16).astype(np.float64), axis, -1)
    blocks = v.reshape(v.shape[:-1] + (-1, 32))
    amax = np.abs(blocks).max(-1, keepdims=True)
    byte = np.maximum(np.where(amax > 0, np.frexp(amax)[1] - 1 + 127, 0) - down, 1)
    scale = np.exp2(byte - 127.0)
    codes = (blocks / scale).astype(np.float32).astype(dtype).astype(np.float64)
    return np.moveaxis((codes * scale).reshape(v.shape), -1, axis)


WIDE = False


def mx_kscale(k):
    if not WIDE:
        return np.ones(k)
    levels = np.array([10, -10, 5, -5, 0])
    if k % 512:
        return np.exp2(np.random.permutation(np.resize(levels, k // 32))).repeat(32)
    a = np.empty((k // 512, 16))
    for p in range(k // 512):
        a[p, :8] = np.random.permutation(np.resize(levels, 8))
        for g in range(8):
            far = levels[np.abs(levels - a[p, g]) >= 10]
            a[p, g + 8] = far[np.random.randint(len(far))]
    return np.exp2(a.ravel()).repeat(32)


def f64(x):
    return np.asarray(x).astype(np.float64)


def striped(idx):
    return np.tile(idx.reshape(-1, 16).T, (8, 1)).astype(np.uint16)


def unstriped(offs):
    return offs[:16].T.reshape(-1).astype(np.int64)


E2M1 = np.array([0.0, 0.5, 1.0, 1.5, 2.0, 3.0, 4.0, 6.0, -0.0, -0.5, -1.0, -1.5, -2.0, -3.0, -4.0, -6.0])


def pack_weight(w, fmt):
    k, n = w.shape
    w = f64(np.asarray(w, np.float32).astype(ml_dtypes.bfloat16)).reshape(k // 32, 32, n)
    amax = np.abs(w).max(1)
    if fmt == "e4m3":
        byte = np.frexp(amax)[1] - 1 + 127 - 7
    else:
        mant, ex = np.frexp(amax / 6.0)
        byte = np.where(mant > 0.5, ex, ex - 1) + 127
    byte = np.clip(np.where(amax > 0, byte, 1), 1, 254)
    scaled = (w * np.exp2(127.0 - byte)[:, None, :]).reshape(k, n).astype(np.float32)
    by_word = np.ascontiguousarray(scaled.reshape(k // 512, 128, 4, n).transpose(0, 1, 3, 2))
    if fmt == "e4m3":
        words = by_word.astype(ml_dtypes.float8_e4m3fn).view(np.uint8)
    else:
        c = by_word.astype(ml_dtypes.float4_e2m1fn).view(np.uint8) & 0xF
        words = (c[..., 0::2] | (c[..., 1::2] << 4)).reshape(k // 512, 128, 2 * n)
    return np.ascontiguousarray(words), np.ascontiguousarray(byte.astype(np.uint8).reshape(k // 512, 16, n))


def unpack_weight(words, scales, fmt):
    g, _, n = scales.shape
    words = np.ascontiguousarray(words).reshape(g, 128, n, -1)
    if fmt == "e4m3":
        vals = words.view(ml_dtypes.float8_e4m3fn).astype(np.float64)
    else:
        nib = np.empty((g, 128, n, 4), np.uint8)
        nib[..., 0::2] = words & 0xF
        nib[..., 1::2] = words >> 4
        vals = E2M1[nib]
    vals = vals * np.repeat(np.exp2(scales.astype(np.float64) - 127.0), 8, axis=1)[..., None]
    return vals.transpose(0, 1, 3, 2).reshape(g * 512, n)


def gelu(v):
    return 0.5 * v * (1.0 + np.tanh(np.sqrt(2.0 / np.pi) * (v + 0.044715 * v**3)))


def striped8(idx):
    return np.concatenate([v.reshape(-1, 16).T for v in idx]).astype(np.uint16)


def unstriped8(offs):
    return np.stack([offs[16 * g:16 * g + 16].T.reshape(-1) for g in range(8)]).astype(np.int64)


def heads(h, wgt, idx8):
    r = np.arange(h.shape[0])
    return wgt[r // 4 % 128] * h[r[:, None], idx8[r % 512 // 64]]


K, H, N, T, S, T2, P = 1024, 1024, 512, 2048, 1024, 2048, 1024

def setup_inputs():
    n = np.random.standard_normal
    s = mx_kscale(K)[:, None]
    u = mx_kscale(H)[:, None]
    tab_words, tab_scales = pack_weight(n((K, T)) * s, "e4m3")
    w2_words, w2_scales = pack_weight(n((H, N)) / np.sqrt(H) / u, "e2m1")
    return {
        "tab_words": tab_words, "tab_scales": tab_scales,
        "w1": (1.4 * n((K, H)) / np.sqrt(K) / s).astype(np.float32),
        "w2_words": w2_words, "w2_scales": w2_scales,
        "w3": (0.8 * n((K, N)) / np.sqrt(K) / s).astype(np.float32),
        "gain": (np.exp(0.3 * n(H)) * u[:, 0]).astype(np.float32),
        "page0": (n((H, T2)) * u).astype(np.float32),
        "load": (0.7 * n((H, P)) * u).astype(np.float32),
        "wgs": np.exp(0.3 * n((128, S))).astype(np.float32),
        "wgt": np.repeat(np.random.uniform(0.5, 2.0, (8, P)), 16, axis=0).astype(np.float32),
        "offs": striped(np.random.permutation(T)[:S]),
        "offs2": striped(np.random.permutation(T2)[:S]),
        "offs3": striped8(np.stack([np.random.permutation(T2)[:P] for _ in range(8)])),
    }

def reference(tab_words, tab_scales, w1, w2_words, w2_scales, w3, gain, page0, load, wgs, wgt, offs, offs2, offs3):
    v = unpack_weight(tab_words, tab_scales, "e4m3")[:, unstriped(offs)]
    w2 = unpack_weight(w2_words, w2_scales, "e2m1")
    w1q = mxq(f64(w1), 0, "e4m3")
    w3q = mxq(f64(w3), 0, "e4m3")
    h = f64(gain)[:, None] * np.tanh(w1q.T @ v)
    page = f64(page0).copy()
    page[:, unstriped(offs2)] = np.tile(f64(wgs), (H // 128, 1)) * h
    x = heads(page, f64(wgt), unstriped8(offs3)) + f64(load)
    xq = mxq(x, 0, "e4m3")
    y = np.tanh(w2.T @ xq)
    return y * np.exp(w3q.T @ v)

@@ -1,0 +1,317 @@
+from contextlib import ExitStack
+
+import concourse.mybir as mybir
+from concourse.masks import make_identity
+
+K, H, N, T, S, T2, M = 1024, 1024, 512, 2048, 1024, 2048, 1024
+FLOPS = 2 * K * H * S + 2 * H * N * M + 2 * K * N * S
+
+F32 = mybir.dt.float32
+BF16 = mybir.dt.bfloat16
+I32 = mybir.dt.int32
+U32 = mybir.dt.uint32
+U16 = mybir.dt.uint16
+U8 = mybir.dt.uint8
+FP8X4 = mybir.dt.float8_e4m3fn_x4
+FP4X4 = mybir.dt.float4_e2m1fn_x4
+ACT = mybir.ActivationFunctionType
+MULT = mybir.AluOpType.mult
+ADD = mybir.AluOpType.add
+
+P = 128
+PACK = 4
+PASS = P * PACK
+PASSES = K // PASS
+PLANES = PASSES * PACK
+BANK = 512
+LIST_COL = 16
+PIECE = 256
+PIECES = M // PIECE
+OUT_TILES = N // P
+HALVES = [(0, BANK), (BANK, BANK)]
+FIRST_CUTS = [(0, 256), (256, 256), (BANK, BANK)]
+
+
+def tile_list_taxel_slip_reading_kernel(
+    tc, tab_words, tab_scales, w1, w2_words, w2_scales, w3, gain, page0, load, wgs, wgt, offs, offs2, offs3, out
+):
+    nc = tc.nc
+    with ExitStack() as ctx:
+        keep = ctx.enter_context(tc.tile_pool(name="keep", bufs=1))
+        ring = ctx.enter_context(tc.tile_pool(name="ring", bufs=2))
+        psum = ctx.enter_context(tc.psum_pool(name="psum", bufs=2))
+
+        def block(shape, dtype, name):
+            return ring.tile(shape, dtype, name=name, tag="block", bufs=12, align_bytes=64)
+
+        def listed(lst, c0, width):
+            return lst[:, c0 // LIST_COL : (c0 + width) // LIST_COL]
+
+        def cols(k):
+            return slice(k * PIECE, (k + 1) * PIECE)
+
+        list1 = keep.tile([P, S // LIST_COL], U16, name="list1")
+        list2 = keep.tile([P, S // LIST_COL], U16, name="list2")
+        list3 = keep.tile([P, M // LIST_COL], U16, name="list3")
+        tab_sc = keep.tile([P, T], U8, name="tab_sc", align_bytes=64)
+        w2_sc = keep.tile([P, PASSES, N], U8, name="w2_sc", align_bytes=64)
+        w2_codes = keep.tile([P, PASSES, 2 * N], U8, name="w2_codes", align_bytes=64)
+        ident = keep.tile([P, P], F32, name="ident")
+        gains = keep.tile([P, PLANES], F32, name="gains")
+        wgt_sb = keep.tile([P, M], F32, name="wgt_sb")
+        v_codes = [keep.tile([P, S], U32, name="v_codes%d" % a, align_bytes=64) for a in range(PASSES)]
+        v_sc = keep.tile([P, S], U8, name="v_sc", align_bytes=64)
+        wgs_sb = [keep.tile([P, S], F32, name="wgs%d" % i, align_bytes=64) for i in range(PACK)]
+        x_sc = [keep.tile([P, M], U8, name="x_sc%d" % b, align_bytes=64) for b in range(PASSES)]
+        grow = [keep.tile([P, OUT_TILES, PIECE], F32, name="grow%d" % k) for k in range(PIECES)]
+        x1 = [keep.tile([P, PIECE * PACK], BF16, name="x1_%d" % k, align_bytes=64) for k in range(PIECES)]
+
+        nc.vector.memset(tab_sc[:].bitcast(I32), 0)
+        nc.vector.memset(w2_sc[:].rearrange("p a n -> p (a n)").bitcast(I32), 0)
+        make_identity(nc, ident[:])
+
+        nc.sync.dma_start(list1[:], offs)
+
+        def load_weight(w, a, c0):
+            raw = block([P, PACK, BANK], F32, "raw")
+            nc.sync.dma_start(
+                out=raw[:], in_=w[a * PASS : (a + 1) * PASS, c0 : c0 + BANK].rearrange("(p j) c -> p j c", j=PACK)
+            )
+            return raw
+
+        def round_weight(raw, dealt):
+            grouped = ring.tile([P, BANK * PACK], BF16, name="grouped", bufs=4, align_bytes=64)
+            if dealt:
+                nc.scalar.copy(
+                    out=grouped[:].rearrange("p (t m j) -> p m t j", t=PACK, j=PACK),
+                    in_=raw[:].rearrange("p j (m t) -> p m t j", t=PACK),
+                )
+            else:
+                nc.scalar.copy(
+                    out=grouped[:].rearrange("p (c t j) -> p c j t", t=PACK, j=PACK),
+                    in_=raw[:].rearrange("p j (c t) -> p c j t", t=PACK),
+                )
+            return grouped
+
+        def quantize_weight(grouped, name):
+            codes = keep.tile([P, BANK], U32, name=name + "_codes", align_bytes=64)
+            scales = keep.tile([P, BANK], U8, name=name + "_sc", align_bytes=64)
+            nc.vector.quantize_mx(out=codes[:].bitcast(FP8X4), scales=scales[:], in_=grouped[:])
+            return codes, scales
+
+        def load_page(plane):
+            page = block([P, T2], F32, "page")
+            b, i = divmod(plane, PACK)
+            nc.sync.dma_start(out=page[:], in_=page0.rearrange("(b p i) t -> b i p t", p=P, i=PACK)[b, i])
+            return page
+
+        def load_wgs(i, c0=0, width=S):
+            rows = wgs.rearrange("(q i) j -> i q j", i=PACK)[i, :, c0 : c0 + width]
+            for quad in range(4):
+                nc.sync.dma_start(out=wgs_sb[i][32 * quad : 32 * quad + 32, c0 : c0 + width], in_=rows)
+
+        def load_pair(b, u):
+            rows = block([P, 2, M], F32, "load_rows")
+            nc.sync.dma_start(
+                out=rows[:], in_=load.rearrange("(b p i) m -> b p i m", p=P, i=PACK)[b, :, 2 * u : 2 * u + 2, :]
+            )
+            return rows
+
+        def table_product(bank, weights, col0, c0, width):
+            for a in range(PASSES):
+                codes, scales = weights[a]
+                nc.tensor.matmul_mx(
+                    out=bank,
+                    lhsT=codes[:, col0 : col0 + P].bitcast(FP8X4),
+                    lhsT_scale=scales[:, col0 : col0 + P],
+                    rhs=v_codes[a][:, c0 : c0 + width].bitcast(FP8X4),
+                    rhs_scale=v_sc[4 * a : P, c0 : c0 + width],
+                    start=(a == 0),
+                    stop=(a == PASSES - 1),
+                )
+
+        def features(w1q, plane):
+            h = keep.tile([P, S], F32, name="h", tag="plane%d" % plane)
+            for c0, width in FIRST_CUTS if plane == 0 else HALVES:
+                bank = psum.tile([P, width], F32, name="h_bank")
+                table_product(bank[:], w1q, plane % PACK * P, c0, width)
+                nc.scalar.activation(out=h[:, c0 : c0 + width], in_=bank[:], func=ACT.Tanh)
+            for c0, width in FIRST_CUTS if plane == 0 else [(0, S)]:
+                part = h[:, c0 : c0 + width]
+                nc.scalar.activation(out=part, in_=part, func=ACT.Copy, scale=gains[:, plane : plane + 1])
+            return h
+
+        def put(plane, h, c0, width):
+            nc.vector.tensor_tensor(
+                pages[plane][:].indirect(listed(list2, c0, width)),
+                h[:, c0 : c0 + width],
+                wgs_sb[plane % PACK][:, c0 : c0 + width],
+                MULT,
+            )
+
+        def pick(dst, plane, c0, width):
+            nc.vector.tensor_tensor(
+                dst, pages[plane][:].indirect(listed(list3, c0, width)), wgt_sb[:, c0 : c0 + width], MULT
+            )
+
+        def sum_by_transposes(x, picked, loaded, k):
+            pairs = len(loaded)
+            slots = [(t, u) for t in range(PIECE // P) for u in range(pairs)]
+            words = psum.tile([P, len(slots), P], F32, name="word_bank")
+            for s0 in range(0, len(slots), 2):
+                sums = psum.tile([P, 2, 2, P], F32, name="sum_bank")
+                for s in range(2):
+                    t, u = slots[s0 + s]
+                    m_cols = slice(k * PIECE + t * P, k * PIECE + (t + 1) * P)
+                    for e in range(2):
+                        nc.tensor.matmul(
+                            sums[:, s, e, :], loaded[u][:, e, m_cols], ident[:], start=True, stop=False, is_transpose=True
+                        )
+                        nc.tensor.matmul(
+                            sums[:, s, e, :], picked[2 * u + e][:, m_cols], ident[:], start=False, stop=True, is_transpose=True
+                        )
+                turned = ring.tile([P, PASS], BF16, name="turned", bufs=3)
+                nc.scalar.copy(
+                    out=turned[:].rearrange("m (s p e) -> m s p e", s=2, e=2),
+                    in_=sums[:].rearrange("m s e p -> m s p e"),
+                )
+                for s in range(2):
+                    nc.tensor.transpose(words[:, s0 + s, :], turned[:].bitcast(F32)[:, s * P : (s + 1) * P], ident[:])
+            nc.scalar.copy(
+                out=x.bitcast(F32).rearrange("p (t m u) -> p t m u", m=P, u=2)[:, :, :, 0:pairs],
+                in_=words[:].rearrange("p (t u) m -> p t m u", u=pairs),
+            )
+
+        def exp_piece(k):
+            for q0 in range(0, OUT_TILES, 2):
+                bank = psum.tile([P, 2, PIECE], F32, name="out_bank")
+                for q in range(2):
+                    table_product(bank[:, q, :], w3q, (q0 + q) * P, k * PIECE, PIECE)
+                nc.scalar.activation(out=grow[k][:, q0 : q0 + 2, :], in_=bank[:], func=ACT.Exp)
+
+        def readings(y, k):
+            for q0 in range(0, OUT_TILES, 2):
+                bank = psum.tile([P, 2, PIECE], F32, name="out_bank")
+                for q in range(2):
+                    n0 = (q0 + q) * P
+                    for b in range(PASSES):
+                        nc.tensor.matmul_mx(
+                            out=bank[:, q, :],
+                            lhsT=w2_codes[:, b, 2 * n0 : 2 * (n0 + P)].bitcast(FP4X4),
+                            lhsT_scale=w2_sc[:, b, n0 : n0 + P],
+                            rhs=x_codes[b][:, cols(k)].bitcast(FP8X4),
+                            rhs_scale=x_sc[b][:, cols(k)],
+                            start=(b == 0),
+                            stop=(b == PASSES - 1),
+                        )
+                nc.scalar.activation(out=y[:, q0 : q0 + 2, :], in_=bank[:], func=ACT.Tanh)
+
+        raw0 = [load_weight(w1, 0, 0)]
+        for quad in range(4):
+            nc.sync.dma_start(
+                out=tab_sc[32 * quad : 32 * quad + 8, :].bitcast(I32),
+                in_=tab_scales[:, 4 * quad : 4 * quad + 4, :].bitcast(I32),
+            )
+        raw0.append(load_weight(w1, 1, 0))
+        tab = []
+        for a in range(PASSES):
+            words = block([P, T], U32, "tab")
+            nc.sync.dma_start(
+                out=words[:].bitcast(I32), in_=tab_words[a].rearrange("p t i -> p (t i)").bitcast(I32)
+            )
+            tab.append(words)
+        nc.sync.dma_start(
+            out=gains[:].rearrange("p (b i) -> p b i", i=PACK), in_=gain.rearrange("(b p i) -> p b i", p=P, i=PACK)
+        )
+        nc.sync.dma_start(list2[:], offs2)
+        load_wgs(0, 0, BANK)
+        pages = [load_page(0)]
+        load_wgs(0, BANK, BANK)
+        load_wgs(1)
+        pages.append(load_page(1))
+        raw1 = [load_weight(w1, 0, BANK)]
+        nc.sync.dma_start(list3[:], offs3)
+        nc.sync.dma_start(out=wgt_sb[:], in_=wgt)
+        load_wgs(2)
+        pages.append(load_page(2))
+        raw1.append(load_weight(w1, 1, BANK))
+        load_wgs(3)
+        pages.append(load_page(3))
+        raw3 = [load_weight(w3, a, 0) for a in range(PASSES)]
+
+        nc.vector.tensor_copy(v_sc[:], tab_sc[:].indirect(list1[:]))
+        w1q = [[quantize_weight(round_weight(raw0[a], True), "w1_0%d" % a) for a in range(PASSES)], []]
+        nc.vector.tensor_copy(v_codes[0][:], tab[0][:].indirect(list1[:]))
+        for c0, width in FIRST_CUTS:
+            nc.vector.tensor_copy(v_codes[1][:, c0 : c0 + width], tab[1][:].indirect(listed(list1, c0, width)))
+
+        pages.extend(load_page(plane) for plane in (4, 5))
+        loaded = [[load_pair(0, u) for u in range(2)]]
+        nc.sync.dma_start(out=w2_codes[:].bitcast(I32), in_=w2_words.rearrange("a p n -> p a n").bitcast(I32))
+        for quad in range(4):
+            nc.sync.dma_start(
+                out=w2_sc[32 * quad : 32 * quad + 4, :, :].bitcast(I32),
+                in_=w2_scales[:, 4 * quad : 4 * quad + 4, :].rearrange("a q n -> q a n").bitcast(I32),
+            )
+
+        hs = [features(w1q[0], plane) for plane in range(PACK)]
+        w1q[1] = [quantize_weight(round_weight(raw1[a], True), "w1_1%d" % a) for a in range(PASSES)]
+        hs.extend(features(w1q[1], plane) for plane in range(PACK, PLANES))
+        w3q = [quantize_weight(round_weight(raw3[a], False), "w3_%d" % a) for a in range(PASSES)]
+
+        picked = []
+        for plane in range(PLANES):
+            if plane == 0:
+                for c0, width in FIRST_CUTS:
+                    put(0, hs[0], c0, width)
+            else:
+                put(plane, hs[plane], 0, S)
+            if 1 <= plane < PLANES - 1:
+                picks = keep.tile([P, M], F32, name="picks", tag="plane%d" % plane)
+                pick(picks[:], plane - 1, 0, M)
+                picked.append(picks)
+            if plane in (1, 2):
+                pages.append(load_page(plane + 5))
+            if plane == 3:
+                loaded.append([load_pair(1, u) for u in range(2)])
+            if plane == 4:
+                for k in range(PIECES):
+                    exp_piece(k)
+                x0 = block([P, M * PACK], BF16, "x0")
+                for k in range(PIECES):
+                    sum_by_transposes(x0[:, k * PIECE * PACK : (k + 1) * PIECE * PACK], picked, loaded[0], k)
+            if plane == 6:
+                x_codes = [
+                    keep.tile([P, M], U32, name="x_codes0", tag="wgs2", align_bytes=64),
+                    keep.tile([P, M], U32, name="x_codes1", align_bytes=64),
+                ]
+                nc.vector.quantize_mx(out=x_codes[0][:].bitcast(FP8X4), scales=x_sc[0][:], in_=x0[:])
+                for k in range(PIECES):
+                    sum_by_transposes(x1[k][:], picked[PACK:], loaded[1][:1], k)
+
+        last = [keep.tile([P, PIECES // 2, 2, PIECE], F32, name="last", tag="plane%d" % plane) for plane in (0, 7)]
+        ys = [block([P, 2, OUT_TILES, PIECE], F32, "y") for half in range(2)]
+
+        def pick_last(k, e):
+            pick(last[k % 2][:, k // 2, e, :], PLANES - 2 + e, k * PIECE, PIECE)
+
+        pick_last(0, 0)
+        pick_last(0, 1)
+        for k in range(PIECES):
+            if k + 1 < PIECES:
+                pick_last(k + 1, 0)
+            nc.vector.tensor_tensor(
+                x1[k][:].rearrange("p (m i) -> p m i", i=PACK)[:, :, 2:PACK],
+                last[k % 2][:, k // 2].rearrange("p e m -> p m e"),
+                loaded[1][1][:, :, cols(k)].rearrange("p e m -> p m e"),
+                ADD,
+            )
+            if k + 1 < PIECES:
+                pick_last(k + 1, 1)
+            nc.vector.quantize_mx(out=x_codes[1][:, cols(k)].bitcast(FP8X4), scales=x_sc[1][:, cols(k)], in_=x1[k][:])
+            readings(ys[k // 2][:, k % 2], k)
+        for k in range(PIECES):
+            for q0, q1 in [(0, 2), (2, OUT_TILES)] if k == PIECES - 1 else [(0, OUT_TILES)]:
+                part = grow[k][:, q0:q1, :]
+                nc.vector.tensor_tensor(part, ys[k // 2][:, k % 2, q0:q1, :], part, MULT)
+                nc.sync.dma_start(out=out.rearrange("(q p) m -> p q m", p=P)[:, q0:q1, cols(k)], in_=part)

@@ -64,7 +64,6 @@ def tile_list_taxel_slip_reading_kernel(
         wgs_sb = [keep.tile([P, S], F32, name="wgs%d" % i, align_bytes=64) for i in range(PACK)]
         x_sc = [keep.tile([P, M], U8, name="x_sc%d" % b, align_bytes=64) for b in range(PASSES)]
         grow = [keep.tile([P, OUT_TILES, PIECE], F32, name="grow%d" % k) for k in range(PIECES)]
-        x1 = [keep.tile([P, PIECE * PACK], BF16, name="x1_%d" % k, align_bytes=64) for k in range(PIECES)]
 
         nc.vector.memset(tab_sc[:].bitcast(I32), 0)
         nc.vector.memset(w2_sc[:].rearrange("p a n -> p (a n)").bitcast(I32), 0)
@@ -79,15 +78,15 @@ def tile_list_taxel_slip_reading_kernel(
             )
             return raw
 
-        def round_weight(raw, dealt):
+        def round_weight(copy, raw, dealt):
             grouped = ring.tile([P, BANK * PACK], BF16, name="grouped", bufs=4, align_bytes=64)
             if dealt:
-                nc.scalar.copy(
+                copy(
                     out=grouped[:].rearrange("p (t m j) -> p m t j", t=PACK, j=PACK),
                     in_=raw[:].rearrange("p j (m t) -> p m t j", t=PACK),
                 )
             else:
-                nc.scalar.copy(
+                copy(
                     out=grouped[:].rearrange("p (c t j) -> p c j t", t=PACK, j=PACK),
                     in_=raw[:].rearrange("p j (c t) -> p c j t", t=PACK),
                 )
@@ -131,7 +130,7 @@ def tile_list_taxel_slip_reading_kernel(
                 )
 
         def features(w1q, plane):
-            h = keep.tile([P, S], F32, name="h", tag="plane%d" % plane)
+            h = keep.tile([P, S], F32, name="h", tag="plane%d" % plane, align_bytes=64)
             for c0, width in FIRST_CUTS if plane == 0 else HALVES:
                 bank = psum.tile([P, width], F32, name="h_bank")
                 table_product(bank[:], w1q, plane % PACK * P, c0, width)
@@ -154,33 +153,35 @@ def tile_list_taxel_slip_reading_kernel(
                 dst, pages[plane][:].indirect(listed(list3, c0, width)), wgt_sb[:, c0 : c0 + width], MULT
             )
 
-        def sum_by_transposes(x, picked, loaded, k):
-            pairs = len(loaded)
-            slots = [(t, u) for t in range(PIECE // P) for u in range(pairs)]
-            words = psum.tile([P, len(slots), P], F32, name="word_bank")
-            for s0 in range(0, len(slots), 2):
+        def turned_sums(b, u):
+            turned = ring.tile([P, M // P, P * 2], BF16, name="turned")
+            for t0 in range(0, M // P, 2):
                 sums = psum.tile([P, 2, 2, P], F32, name="sum_bank")
-                for s in range(2):
-                    t, u = slots[s0 + s]
-                    m_cols = slice(k * PIECE + t * P, k * PIECE + (t + 1) * P)
+                for t in range(2):
+                    m_cols = slice((t0 + t) * P, (t0 + t + 1) * P)
                     for e in range(2):
-                        nc.tensor.matmul(
-                            sums[:, s, e, :], loaded[u][:, e, m_cols], ident[:], start=True, stop=False, is_transpose=True
-                        )
-                        nc.tensor.matmul(
-                            sums[:, s, e, :], picked[2 * u + e][:, m_cols], ident[:], start=False, stop=True, is_transpose=True
-                        )
-                turned = ring.tile([P, PASS], BF16, name="turned", bufs=3)
+                        terms = (loaded[b][u][:, e, m_cols], picked[PACK * b + 2 * u + e][:, m_cols])
+                        for n, term in enumerate(terms):
+                            nc.tensor.matmul(
+                                sums[:, t, e, :], term, ident[:], start=(n == 0), stop=(n == 1), is_transpose=True
+                            )
                 nc.scalar.copy(
-                    out=turned[:].rearrange("m (s p e) -> m s p e", s=2, e=2),
-                    in_=sums[:].rearrange("m s e p -> m s p e"),
+                    out=turned[:, t0 : t0 + 2, :].rearrange("m t (p e) -> m t p e", e=2),
+                    in_=sums[:].rearrange("m t e p -> m t p e"),
                 )
-                for s in range(2):
-                    nc.tensor.transpose(words[:, s0 + s, :], turned[:].bitcast(F32)[:, s * P : (s + 1) * P], ident[:])
-            nc.scalar.copy(
-                out=x.bitcast(F32).rearrange("p (t m u) -> p t m u", m=P, u=2)[:, :, :, 0:pairs],
-                in_=words[:].rearrange("p (t u) m -> p t m u", u=pairs),
-            )
+            return turned
+
+        def turn_back(pairs, k):
+            words = psum.tile([P, len(pairs), PIECE], F32, name="word_bank")
+            for u, turned in enumerate(pairs):
+                for t in range(PIECE // P):
+                    nc.tensor.transpose(
+                        words[:, u, t * P : (t + 1) * P], turned[:, k * PIECE // P + t, :].bitcast(F32), ident[:]
+                    )
+            return words
+
+        def weave(x, words):
+            nc.scalar.copy(out=x.bitcast(F32).rearrange("p (m u) -> p m u", u=2), in_=words.rearrange("p u m -> p m u"))
 
         def exp_piece(k):
             for q0 in range(0, OUT_TILES, 2):
@@ -235,18 +236,21 @@ def tile_list_taxel_slip_reading_kernel(
         load_wgs(2)
         pages.append(load_page(2))
         raw1.append(load_weight(w1, 1, BANK))
+        raw3 = [load_weight(w3, a, 0) for a in range(PASSES)]
         load_wgs(3)
         pages.append(load_page(3))
-        raw3 = [load_weight(w3, a, 0) for a in range(PASSES)]
 
         nc.vector.tensor_copy(v_sc[:], tab_sc[:].indirect(list1[:]))
-        w1q = [[quantize_weight(round_weight(raw0[a], True), "w1_0%d" % a) for a in range(PASSES)], []]
+        first_copies = (nc.vector.tensor_copy, nc.scalar.copy)
+        w1q = [[quantize_weight(round_weight(first_copies[a], raw0[a], True), "w1_0%d" % a) for a in range(PASSES)]]
         nc.vector.tensor_copy(v_codes[0][:], tab[0][:].indirect(list1[:]))
         for c0, width in FIRST_CUTS:
             nc.vector.tensor_copy(v_codes[1][:, c0 : c0 + width], tab[1][:].indirect(listed(list1, c0, width)))
 
-        pages.extend(load_page(plane) for plane in (4, 5))
-        loaded = [[load_pair(0, u) for u in range(2)]]
+        loaded = [[], []]
+        for u in range(2):
+            loaded[0].append(load_pair(0, u))
+            pages.append(load_page(PACK + u))
         nc.sync.dma_start(out=w2_codes[:].bitcast(I32), in_=w2_words.rearrange("a p n -> p a n").bitcast(I32))
         for quad in range(4):
             nc.sync.dma_start(
@@ -255,9 +259,9 @@ def tile_list_taxel_slip_reading_kernel(
             )
 
         hs = [features(w1q[0], plane) for plane in range(PACK)]
-        w1q[1] = [quantize_weight(round_weight(raw1[a], True), "w1_1%d" % a) for a in range(PASSES)]
+        w1q.append([quantize_weight(round_weight(nc.scalar.copy, raw1[a], True), "w1_1%d" % a) for a in range(PASSES)])
+        w3q = [quantize_weight(round_weight(nc.scalar.copy, raw3[a], False), "w3_%d" % a) for a in range(PASSES)]
         hs.extend(features(w1q[1], plane) for plane in range(PACK, PLANES))
-        w3q = [quantize_weight(round_weight(raw3[a], False), "w3_%d" % a) for a in range(PASSES)]
 
         picked = []
         for plane in range(PLANES):
@@ -267,49 +271,59 @@ def tile_list_taxel_slip_reading_kernel(
             else:
                 put(plane, hs[plane], 0, S)
             if 1 <= plane < PLANES - 1:
-                picks = keep.tile([P, M], F32, name="picks", tag="plane%d" % plane)
+                picks = keep.tile([P, M], F32, name="picks", tag="plane%d" % plane, align_bytes=64)
                 pick(picks[:], plane - 1, 0, M)
                 picked.append(picks)
             if plane in (1, 2):
                 pages.append(load_page(plane + 5))
-            if plane == 3:
-                loaded.append([load_pair(1, u) for u in range(2)])
-            if plane == 4:
+                loaded[1].append(load_pair(1, plane - 1))
+            if plane == 2:
+                low = turned_sums(0, 0)
                 for k in range(PIECES):
                     exp_piece(k)
+            if plane == 4:
+                high = turned_sums(0, 1)
                 x0 = block([P, M * PACK], BF16, "x0")
                 for k in range(PIECES):
-                    sum_by_transposes(x0[:, k * PIECE * PACK : (k + 1) * PIECE * PACK], picked, loaded[0], k)
+                    weave(x0[:, k * PIECE * PACK : (k + 1) * PIECE * PACK], turn_back([low, high], k)[:])
             if plane == 6:
-                x_codes = [
-                    keep.tile([P, M], U32, name="x_codes0", tag="wgs2", align_bytes=64),
-                    keep.tile([P, M], U32, name="x_codes1", align_bytes=64),
-                ]
-                nc.vector.quantize_mx(out=x_codes[0][:].bitcast(FP8X4), scales=x_sc[0][:], in_=x0[:])
+                low = turned_sums(1, 0)
+                halves = []
                 for k in range(PIECES):
-                    sum_by_transposes(x1[k][:], picked[PACK:], loaded[1][:1], k)
+                    half = keep.tile([P, 2, PIECE], F32, name="half", tag="plane%d" % (k + 1), align_bytes=64)
+                    nc.scalar.copy(out=half[:, 0, :], in_=turn_back([low], k)[:, 0, :])
+                    halves.append(half)
 
-        last = [keep.tile([P, PIECES // 2, 2, PIECE], F32, name="last", tag="plane%d" % plane) for plane in (0, 7)]
+        x_codes = [
+            keep.tile([P, M], U32, name="x_codes0", tag="wgs3", align_bytes=64),
+            keep.tile([P, M], U32, name="x_codes1", align_bytes=64),
+        ]
         ys = [block([P, 2, OUT_TILES, PIECE], F32, "y") for half in range(2)]
+        last_tags = ["plane0", "plane7", "x1_0", "x1_1"]
+        x1 = []
 
-        def pick_last(k, e):
-            pick(last[k % 2][:, k // 2, e, :], PLANES - 2 + e, k * PIECE, PIECE)
+        def quantize_last(k):
+            nc.vector.quantize_mx(out=x_codes[1][:, cols(k)].bitcast(FP8X4), scales=x_sc[1][:, cols(k)], in_=x1[k][:])
+            readings(ys[k // 2][:, k % 2], k)
 
-        pick_last(0, 0)
-        pick_last(0, 1)
         for k in range(PIECES):
-            if k + 1 < PIECES:
-                pick_last(k + 1, 0)
+            last = keep.tile([P, 2, PIECE], F32, name="last", tag=last_tags[k], align_bytes=64)
+            for e in range(2):
+                pick(last[:, e, :], PLANES - 2 + e, k * PIECE, PIECE)
+            if k == 0:
+                nc.vector.quantize_mx(out=x_codes[0][:].bitcast(FP8X4), scales=x_sc[0][:], in_=x0[:])
+            else:
+                quantize_last(k - 1)
             nc.vector.tensor_tensor(
-                x1[k][:].rearrange("p (m i) -> p m i", i=PACK)[:, :, 2:PACK],
-                last[k % 2][:, k // 2].rearrange("p e m -> p m e"),
+                halves[k][:, 1, :].bitcast(BF16).rearrange("p (m e) -> p m e", e=2),
+                last[:].rearrange("p e m -> p m e"),
                 loaded[1][1][:, :, cols(k)].rearrange("p e m -> p m e"),
                 ADD,
             )
-            if k + 1 < PIECES:
-                pick_last(k + 1, 1)
-            nc.vector.quantize_mx(out=x_codes[1][:, cols(k)].bitcast(FP8X4), scales=x_sc[1][:, cols(k)], in_=x1[k][:])
-            readings(ys[k // 2][:, k % 2], k)
+            x = keep.tile([P, PIECE * PACK], BF16, name="x1_%d" % k, align_bytes=64)
+            weave(x[:], halves[k][:])
+            x1.append(x)
+        quantize_last(PIECES - 1)
         for k in range(PIECES):
             for q0, q1 in [(0, 2), (2, OUT_TILES)] if k == PIECES - 1 else [(0, OUT_TILES)]:
                 part = grow[k][:, q0:q1, :]

@@ -78,18 +78,17 @@ def tile_list_taxel_slip_reading_kernel(
             )
             return raw
 
-        def round_weight(copy, raw, dealt):
+        def round_weight(copies, raw, dealt):
             grouped = ring.tile([P, BANK * PACK], BF16, name="grouped", bufs=4, align_bytes=64)
             if dealt:
-                copy(
-                    out=grouped[:].rearrange("p (t m j) -> p m t j", t=PACK, j=PACK),
-                    in_=raw[:].rearrange("p j (m t) -> p m t j", t=PACK),
-                )
+                dst = grouped[:].rearrange("p (t m j) -> p m t j", t=PACK, j=PACK)
+                src = raw[:].rearrange("p j (m t) -> p m t j", t=PACK)
             else:
-                copy(
-                    out=grouped[:].rearrange("p (c t j) -> p c j t", t=PACK, j=PACK),
-                    in_=raw[:].rearrange("p j (c t) -> p c j t", t=PACK),
-                )
+                dst = grouped[:].rearrange("p (c t j) -> p c j t", t=PACK, j=PACK)
+                src = raw[:].rearrange("p j (c t) -> p c j t", t=PACK)
+            share = P // len(copies)
+            for n, copy in enumerate(copies):
+                copy(out=dst[:, n * share : (n + 1) * share], in_=src[:, n * share : (n + 1) * share])
             return grouped
 
         def quantize_weight(grouped, name):
@@ -190,22 +189,17 @@ def tile_list_taxel_slip_reading_kernel(
                     table_product(bank[:, q, :], w3q, (q0 + q) * P, k * PIECE, PIECE)
                 nc.scalar.activation(out=grow[k][:, q0 : q0 + 2, :], in_=bank[:], func=ACT.Exp)
 
-        def readings(y, k):
-            for q0 in range(0, OUT_TILES, 2):
-                bank = psum.tile([P, 2, PIECE], F32, name="out_bank")
-                for q in range(2):
-                    n0 = (q0 + q) * P
-                    for b in range(PASSES):
-                        nc.tensor.matmul_mx(
-                            out=bank[:, q, :],
-                            lhsT=w2_codes[:, b, 2 * n0 : 2 * (n0 + P)].bitcast(FP4X4),
-                            lhsT_scale=w2_sc[:, b, n0 : n0 + P],
-                            rhs=x_codes[b][:, cols(k)].bitcast(FP8X4),
-                            rhs_scale=x_sc[b][:, cols(k)],
-                            start=(b == 0),
-                            stop=(b == PASSES - 1),
-                        )
-                nc.scalar.activation(out=y[:, q0 : q0 + 2, :], in_=bank[:], func=ACT.Tanh)
+        def score_pass(b, banks, k):
+            for q in range(OUT_TILES):
+                nc.tensor.matmul_mx(
+                    out=banks[q // 2][:, q % 2, :],
+                    lhsT=w2_codes[:, b, 2 * q * P : 2 * (q + 1) * P].bitcast(FP4X4),
+                    lhsT_scale=w2_sc[:, b, q * P : (q + 1) * P],
+                    rhs=x_codes[b][:, cols(k)].bitcast(FP8X4),
+                    rhs_scale=x_sc[b][:, cols(k)],
+                    start=(b == 0 and q % 2 == 0),
+                    stop=(b == PASSES - 1 and q % 2 == 1),
+                )
 
         raw0 = [load_weight(w1, 0, 0)]
         for quad in range(4):
@@ -225,8 +219,8 @@ def tile_list_taxel_slip_reading_kernel(
             out=gains[:].rearrange("p (b i) -> p b i", i=PACK), in_=gain.rearrange("(b p i) -> p b i", p=P, i=PACK)
         )
         nc.sync.dma_start(list2[:], offs2)
-        load_wgs(0, 0, BANK)
         pages = [load_page(0)]
+        load_wgs(0, 0, BANK)
         load_wgs(0, BANK, BANK)
         load_wgs(1)
         pages.append(load_page(1))
@@ -241,7 +235,7 @@ def tile_list_taxel_slip_reading_kernel(
         pages.append(load_page(3))
 
         nc.vector.tensor_copy(v_sc[:], tab_sc[:].indirect(list1[:]))
-        first_copies = (nc.vector.tensor_copy, nc.scalar.copy)
+        first_copies = ([nc.vector.tensor_copy], [nc.vector.tensor_copy, nc.scalar.copy])
         w1q = [[quantize_weight(round_weight(first_copies[a], raw0[a], True), "w1_0%d" % a) for a in range(PASSES)]]
         nc.vector.tensor_copy(v_codes[0][:], tab[0][:].indirect(list1[:]))
         for c0, width in FIRST_CUTS:
@@ -259,8 +253,8 @@ def tile_list_taxel_slip_reading_kernel(
             )
 
         hs = [features(w1q[0], plane) for plane in range(PACK)]
-        w1q.append([quantize_weight(round_weight(nc.scalar.copy, raw1[a], True), "w1_1%d" % a) for a in range(PASSES)])
-        w3q = [quantize_weight(round_weight(nc.scalar.copy, raw3[a], False), "w3_%d" % a) for a in range(PASSES)]
+        w1q.append([quantize_weight(round_weight([nc.scalar.copy], raw1[a], True), "w1_1%d" % a) for a in range(PASSES)])
+        w3q = [quantize_weight(round_weight([nc.scalar.copy], raw3[a], False), "w3_%d" % a) for a in range(PASSES)]
         hs.extend(features(w1q[1], plane) for plane in range(PACK, PLANES))
 
         picked = []
@@ -298,22 +292,43 @@ def tile_list_taxel_slip_reading_kernel(
             keep.tile([P, M], U32, name="x_codes0", tag="wgs3", align_bytes=64),
             keep.tile([P, M], U32, name="x_codes1", align_bytes=64),
         ]
-        ys = [block([P, 2, OUT_TILES, PIECE], F32, "y") for half in range(2)]
-        last_tags = ["plane0", "plane7", "x1_0", "x1_1"]
-        x1 = []
 
-        def quantize_last(k):
+        last_tags = ["plane0", "plane7", "x1_0", "wgs0"]
+        y_tags = ["wgs0", "wgs1", "plane5", "plane6"]
+        x1 = []
+        ys = []
+
+        def finish_scores(k):
             nc.vector.quantize_mx(out=x_codes[1][:, cols(k)].bitcast(FP8X4), scales=x_sc[1][:, cols(k)], in_=x1[k][:])
-            readings(ys[k // 2][:, k % 2], k)
+            if k == PIECES - 1:
+                banks = last_banks
+            else:
+                banks = [psum.tile([P, 2, PIECE], F32, name="out_bank") for half in range(2)]
+                score_pass(0, banks, k)
+            score_pass(1, banks, k)
+            y = keep.tile([P, OUT_TILES, PIECE], F32, name="y", tag=y_tags[k], align_bytes=64)
+            for half in range(2):
+                nc.scalar.activation(out=y[:, 2 * half : 2 * half + 2, :], in_=banks[half][:], func=ACT.Tanh)
+            ys.append(y)
+
+        def store(k):
+            for q0, q1 in [(0, 2), (2, OUT_TILES)] if k == PIECES - 1 else [(0, OUT_TILES)]:
+                part = grow[k][:, q0:q1, :]
+                nc.vector.tensor_tensor(part, ys[k][:, q0:q1, :], part, MULT)
+                nc.sync.dma_start(out=out.rearrange("(q p) m -> p q m", p=P)[:, q0:q1, cols(k)], in_=part)
 
         for k in range(PIECES):
+            if k == PIECES - 1:
+                store(0)
             last = keep.tile([P, 2, PIECE], F32, name="last", tag=last_tags[k], align_bytes=64)
             for e in range(2):
                 pick(last[:, e, :], PLANES - 2 + e, k * PIECE, PIECE)
             if k == 0:
                 nc.vector.quantize_mx(out=x_codes[0][:].bitcast(FP8X4), scales=x_sc[0][:], in_=x0[:])
+                last_banks = [psum.tile([P, 2, PIECE], F32, name="h_bank") for half in range(2)]
+                score_pass(0, last_banks, PIECES - 1)
             else:
-                quantize_last(k - 1)
+                finish_scores(k - 1)
             nc.vector.tensor_tensor(
                 halves[k][:, 1, :].bitcast(BF16).rearrange("p (m e) -> p m e", e=2),
                 last[:].rearrange("p e m -> p m e"),
@@ -323,9 +338,7 @@ def tile_list_taxel_slip_reading_kernel(
             x = keep.tile([P, PIECE * PACK], BF16, name="x1_%d" % k, align_bytes=64)
             weave(x[:], halves[k][:])
             x1.append(x)
-        quantize_last(PIECES - 1)
-        for k in range(PIECES):
-            for q0, q1 in [(0, 2), (2, OUT_TILES)] if k == PIECES - 1 else [(0, OUT_TILES)]:
-                part = grow[k][:, q0:q1, :]
-                nc.vector.tensor_tensor(part, ys[k // 2][:, k % 2, q0:q1, :], part, MULT)
-                nc.sync.dma_start(out=out.rearrange("(q p) m -> p q m", p=P)[:, q0:q1, cols(k)], in_=part)
+        store(1)
+        finish_scores(PIECES - 1)
+        for k in range(2, PIECES):
+            store(k)

from contextlib import ExitStack

import concourse.mybir as mybir
from concourse.masks import make_identity

K, H, N, T, S, T2, M = 1024, 1024, 512, 2048, 1024, 2048, 1024
FLOPS = 2 * K * H * S + 2 * H * N * M + 2 * K * N * S

F32 = mybir.dt.float32
BF16 = mybir.dt.bfloat16
I32 = mybir.dt.int32
U32 = mybir.dt.uint32
U16 = mybir.dt.uint16
U8 = mybir.dt.uint8
FP8X4 = mybir.dt.float8_e4m3fn_x4
FP4X4 = mybir.dt.float4_e2m1fn_x4
ACT = mybir.ActivationFunctionType
MULT = mybir.AluOpType.mult
ADD = mybir.AluOpType.add

P = 128
PACK = 4
PASS = P * PACK
PASSES = K // PASS
PLANES = PASSES * PACK
BANK = 512
LIST_COL = 16
PIECE = 256
PIECES = M // PIECE
OUT_TILES = N // P
HALVES = [(0, BANK), (BANK, BANK)]
FIRST_CUTS = [(0, 256), (256, 256), (BANK, BANK)]


def tile_list_taxel_slip_reading_kernel(
    tc, tab_words, tab_scales, w1, w2_words, w2_scales, w3, gain, page0, load, wgs, wgt, offs, offs2, offs3, out
):
    nc = tc.nc
    with ExitStack() as ctx:
        keep = ctx.enter_context(tc.tile_pool(name="keep", bufs=1))
        ring = ctx.enter_context(tc.tile_pool(name="ring", bufs=2))
        psum = ctx.enter_context(tc.psum_pool(name="psum", bufs=2))

        def block(shape, dtype, name):
            return ring.tile(shape, dtype, name=name, tag="block", bufs=12, align_bytes=64)

        def listed(lst, c0, width):
            return lst[:, c0 // LIST_COL : (c0 + width) // LIST_COL]

        def cols(k):
            return slice(k * PIECE, (k + 1) * PIECE)

        list1 = keep.tile([P, S // LIST_COL], U16, name="list1")
        list2 = keep.tile([P, S // LIST_COL], U16, name="list2")
        list3 = keep.tile([P, M // LIST_COL], U16, name="list3")
        tab_sc = keep.tile([P, T], U8, name="tab_sc", align_bytes=64)
        w2_sc = keep.tile([P, PASSES, N], U8, name="w2_sc", align_bytes=64)
        w2_codes = keep.tile([P, PASSES, 2 * N], U8, name="w2_codes", align_bytes=64)
        ident = keep.tile([P, P], F32, name="ident")
        gains = keep.tile([P, PLANES], F32, name="gains")
        wgt_sb = keep.tile([P, M], F32, name="wgt_sb")
        v_codes = [keep.tile([P, S], U32, name="v_codes%d" % a, align_bytes=64) for a in range(PASSES)]
        v_sc = keep.tile([P, S], U8, name="v_sc", align_bytes=64)
        wgs_sb = [keep.tile([P, S], F32, name="wgs%d" % i, align_bytes=64) for i in range(PACK)]
        x_sc = [keep.tile([P, M], U8, name="x_sc%d" % b, align_bytes=64) for b in range(PASSES)]
        grow = [keep.tile([P, OUT_TILES, PIECE], F32, name="grow%d" % k) for k in range(PIECES)]

        nc.vector.memset(tab_sc[:].bitcast(I32), 0)
        nc.vector.memset(w2_sc[:].rearrange("p a n -> p (a n)").bitcast(I32), 0)
        make_identity(nc, ident[:])

        nc.sync.dma_start(list1[:], offs)

        def load_weight(w, a, c0):
            raw = block([P, PACK, BANK], F32, "raw")
            nc.sync.dma_start(
                out=raw[:], in_=w[a * PASS : (a + 1) * PASS, c0 : c0 + BANK].rearrange("(p j) c -> p j c", j=PACK)
            )
            return raw

        def round_weight(copies, raw, dealt):
            grouped = ring.tile([P, BANK * PACK], BF16, name="grouped", bufs=4, align_bytes=64)
            if dealt:
                dst = grouped[:].rearrange("p (t m j) -> p m t j", t=PACK, j=PACK)
                src = raw[:].rearrange("p j (m t) -> p m t j", t=PACK)
            else:
                dst = grouped[:].rearrange("p (c t j) -> p c j t", t=PACK, j=PACK)
                src = raw[:].rearrange("p j (c t) -> p c j t", t=PACK)
            share = P // len(copies)
            for n, copy in enumerate(copies):
                copy(out=dst[:, n * share : (n + 1) * share], in_=src[:, n * share : (n + 1) * share])
            return grouped

        def quantize_weight(grouped, name):
            codes = keep.tile([P, BANK], U32, name=name + "_codes", align_bytes=64)
            scales = keep.tile([P, BANK], U8, name=name + "_sc", align_bytes=64)
            nc.vector.quantize_mx(out=codes[:].bitcast(FP8X4), scales=scales[:], in_=grouped[:])
            return codes, scales

        def load_page(plane):
            page = block([P, T2], F32, "page")
            b, i = divmod(plane, PACK)
            nc.sync.dma_start(out=page[:], in_=page0.rearrange("(b p i) t -> b i p t", p=P, i=PACK)[b, i])
            return page

        def load_wgs(i, c0=0, width=S):
            rows = wgs.rearrange("(q i) j -> i q j", i=PACK)[i, :, c0 : c0 + width]
            for quad in range(4):
                nc.sync.dma_start(out=wgs_sb[i][32 * quad : 32 * quad + 32, c0 : c0 + width], in_=rows)

        def load_pair(b, u):
            rows = block([P, 2, M], F32, "load_rows")
            nc.sync.dma_start(
                out=rows[:], in_=load.rearrange("(b p i) m -> b p i m", p=P, i=PACK)[b, :, 2 * u : 2 * u + 2, :]
            )
            return rows

        def table_product(bank, weights, col0, c0, width):
            for a in range(PASSES):
                codes, scales = weights[a]
                nc.tensor.matmul_mx(
                    out=bank,
                    lhsT=codes[:, col0 : col0 + P].bitcast(FP8X4),
                    lhsT_scale=scales[:, col0 : col0 + P],
                    rhs=v_codes[a][:, c0 : c0 + width].bitcast(FP8X4),
                    rhs_scale=v_sc[4 * a : P, c0 : c0 + width],
                    start=(a == 0),
                    stop=(a == PASSES - 1),
                )

        def features(w1q, plane):
            h = keep.tile([P, S], F32, name="h", tag="plane%d" % plane, align_bytes=64)
            for c0, width in FIRST_CUTS if plane == 0 else HALVES:
                bank = psum.tile([P, width], F32, name="h_bank")
                table_product(bank[:], w1q, plane % PACK * P, c0, width)
                nc.scalar.activation(out=h[:, c0 : c0 + width], in_=bank[:], func=ACT.Tanh)
            for c0, width in FIRST_CUTS if plane == 0 else [(0, S)]:
                part = h[:, c0 : c0 + width]
                nc.scalar.activation(out=part, in_=part, func=ACT.Copy, scale=gains[:, plane : plane + 1])
            return h

        def put(plane, h, c0, width):
            nc.vector.tensor_tensor(
                pages[plane][:].indirect(listed(list2, c0, width)),
                h[:, c0 : c0 + width],
                wgs_sb[plane % PACK][:, c0 : c0 + width],
                MULT,
            )

        def pick(dst, plane, c0, width):
            nc.vector.tensor_tensor(
                dst, pages[plane][:].indirect(listed(list3, c0, width)), wgt_sb[:, c0 : c0 + width], MULT
            )

        def turned_sums(b, u):
            turned = ring.tile([P, M // P, P * 2], BF16, name="turned")
            for t0 in range(0, M // P, 2):
                sums = psum.tile([P, 2, 2, P], F32, name="sum_bank")
                for t in range(2):
                    m_cols = slice((t0 + t) * P, (t0 + t + 1) * P)
                    for e in range(2):
                        terms = (loaded[b][u][:, e, m_cols], picked[PACK * b + 2 * u + e][:, m_cols])
                        for n, term in enumerate(terms):
                            nc.tensor.matmul(
                                sums[:, t, e, :], term, ident[:], start=(n == 0), stop=(n == 1), is_transpose=True
                            )
                nc.scalar.copy(
                    out=turned[:, t0 : t0 + 2, :].rearrange("m t (p e) -> m t p e", e=2),
                    in_=sums[:].rearrange("m t e p -> m t p e"),
                )
            return turned

        def turn_back(pairs, k):
            words = psum.tile([P, len(pairs), PIECE], F32, name="word_bank")
            for u, turned in enumerate(pairs):
                for t in range(PIECE // P):
                    nc.tensor.transpose(
                        words[:, u, t * P : (t + 1) * P], turned[:, k * PIECE // P + t, :].bitcast(F32), ident[:]
                    )
            return words

        def weave(x, words):
            nc.scalar.copy(out=x.bitcast(F32).rearrange("p (m u) -> p m u", u=2), in_=words.rearrange("p u m -> p m u"))

        def exp_piece(k):
            for q0 in range(0, OUT_TILES, 2):
                bank = psum.tile([P, 2, PIECE], F32, name="out_bank")
                for q in range(2):
                    table_product(bank[:, q, :], w3q, (q0 + q) * P, k * PIECE, PIECE)
                nc.scalar.activation(out=grow[k][:, q0 : q0 + 2, :], in_=bank[:], func=ACT.Exp)

        def score_pass(b, banks, k):
            for q in range(OUT_TILES):
                nc.tensor.matmul_mx(
                    out=banks[q // 2][:, q % 2, :],
                    lhsT=w2_codes[:, b, 2 * q * P : 2 * (q + 1) * P].bitcast(FP4X4),
                    lhsT_scale=w2_sc[:, b, q * P : (q + 1) * P],
                    rhs=x_codes[b][:, cols(k)].bitcast(FP8X4),
                    rhs_scale=x_sc[b][:, cols(k)],
                    start=(b == 0 and q % 2 == 0),
                    stop=(b == PASSES - 1 and q % 2 == 1),
                )

        raw0 = [load_weight(w1, 0, 0)]
        for quad in range(4):
            nc.sync.dma_start(
                out=tab_sc[32 * quad : 32 * quad + 8, :].bitcast(I32),
                in_=tab_scales[:, 4 * quad : 4 * quad + 4, :].bitcast(I32),
            )
        raw0.append(load_weight(w1, 1, 0))
        tab = []
        for a in range(PASSES):
            words = block([P, T], U32, "tab")
            nc.sync.dma_start(
                out=words[:].bitcast(I32), in_=tab_words[a].rearrange("p t i -> p (t i)").bitcast(I32)
            )
            tab.append(words)
        nc.sync.dma_start(
            out=gains[:].rearrange("p (b i) -> p b i", i=PACK), in_=gain.rearrange("(b p i) -> p b i", p=P, i=PACK)
        )
        nc.sync.dma_start(list2[:], offs2)
        pages = [load_page(0)]
        load_wgs(0, 0, BANK)
        load_wgs(0, BANK, BANK)
        load_wgs(1)
        pages.append(load_page(1))
        raw1 = [load_weight(w1, 0, BANK)]
        nc.sync.dma_start(list3[:], offs3)
        nc.sync.dma_start(out=wgt_sb[:], in_=wgt)
        load_wgs(2)
        pages.append(load_page(2))
        raw1.append(load_weight(w1, 1, BANK))
        raw3 = [load_weight(w3, a, 0) for a in range(PASSES)]
        load_wgs(3)
        pages.append(load_page(3))

        nc.vector.tensor_copy(v_sc[:], tab_sc[:].indirect(list1[:]))
        first_copies = ([nc.vector.tensor_copy], [nc.vector.tensor_copy, nc.scalar.copy])
        w1q = [[quantize_weight(round_weight(first_copies[a], raw0[a], True), "w1_0%d" % a) for a in range(PASSES)]]
        nc.vector.tensor_copy(v_codes[0][:], tab[0][:].indirect(list1[:]))
        for c0, width in FIRST_CUTS:
            nc.vector.tensor_copy(v_codes[1][:, c0 : c0 + width], tab[1][:].indirect(listed(list1, c0, width)))

        loaded = [[], []]
        for u in range(2):
            loaded[0].append(load_pair(0, u))
            pages.append(load_page(PACK + u))
        nc.sync.dma_start(out=w2_codes[:].bitcast(I32), in_=w2_words.rearrange("a p n -> p a n").bitcast(I32))
        for quad in range(4):
            nc.sync.dma_start(
                out=w2_sc[32 * quad : 32 * quad + 4, :, :].bitcast(I32),
                in_=w2_scales[:, 4 * quad : 4 * quad + 4, :].rearrange("a q n -> q a n").bitcast(I32),
            )

        hs = [features(w1q[0], plane) for plane in range(PACK)]
        w1q.append([quantize_weight(round_weight([nc.scalar.copy], raw1[a], True), "w1_1%d" % a) for a in range(PASSES)])
        w3q = [quantize_weight(round_weight([nc.scalar.copy], raw3[a], False), "w3_%d" % a) for a in range(PASSES)]
        hs.extend(features(w1q[1], plane) for plane in range(PACK, PLANES))

        picked = []
        for plane in range(PLANES):
            if plane == 0:
                for c0, width in FIRST_CUTS:
                    put(0, hs[0], c0, width)
            else:
                put(plane, hs[plane], 0, S)
            if 1 <= plane < PLANES - 1:
                picks = keep.tile([P, M], F32, name="picks", tag="plane%d" % plane, align_bytes=64)
                pick(picks[:], plane - 1, 0, M)
                picked.append(picks)
            if plane in (1, 2):
                pages.append(load_page(plane + 5))
                loaded[1].append(load_pair(1, plane - 1))
            if plane == 2:
                low = turned_sums(0, 0)
                for k in range(PIECES):
                    exp_piece(k)
            if plane == 4:
                high = turned_sums(0, 1)
                x0 = block([P, M * PACK], BF16, "x0")
                for k in range(PIECES):
                    weave(x0[:, k * PIECE * PACK : (k + 1) * PIECE * PACK], turn_back([low, high], k)[:])
            if plane == 6:
                low = turned_sums(1, 0)
                halves = []
                for k in range(PIECES):
                    half = keep.tile([P, 2, PIECE], F32, name="half", tag="plane%d" % (k + 1), align_bytes=64)
                    nc.scalar.copy(out=half[:, 0, :], in_=turn_back([low], k)[:, 0, :])
                    halves.append(half)

        x_codes = [
            keep.tile([P, M], U32, name="x_codes0", tag="wgs3", align_bytes=64),
            keep.tile([P, M], U32, name="x_codes1", align_bytes=64),
        ]

        last_tags = ["plane0", "plane7", "x1_0", "wgs0"]
        y_tags = ["wgs0", "wgs1", "plane5", "plane6"]
        x1 = []
        ys = []

        def finish_scores(k):
            nc.vector.quantize_mx(out=x_codes[1][:, cols(k)].bitcast(FP8X4), scales=x_sc[1][:, cols(k)], in_=x1[k][:])
            if k == PIECES - 1:
                banks = last_banks
            else:
                banks = [psum.tile([P, 2, PIECE], F32, name="out_bank") for half in range(2)]
                score_pass(0, banks, k)
            score_pass(1, banks, k)
            y = keep.tile([P, OUT_TILES, PIECE], F32, name="y", tag=y_tags[k], align_bytes=64)
            for half in range(2):
                nc.scalar.activation(out=y[:, 2 * half : 2 * half + 2, :], in_=banks[half][:], func=ACT.Tanh)
            ys.append(y)

        def store(k):
            for q0, q1 in [(0, 2), (2, OUT_TILES)] if k == PIECES - 1 else [(0, OUT_TILES)]:
                part = grow[k][:, q0:q1, :]
                nc.vector.tensor_tensor(part, ys[k][:, q0:q1, :], part, MULT)
                nc.sync.dma_start(out=out.rearrange("(q p) m -> p q m", p=P)[:, q0:q1, cols(k)], in_=part)

        for k in range(PIECES):
            if k == PIECES - 1:
                store(0)
            last = keep.tile([P, 2, PIECE], F32, name="last", tag=last_tags[k], align_bytes=64)
            for e in range(2):
                pick(last[:, e, :], PLANES - 2 + e, k * PIECE, PIECE)
            if k == 0:
                nc.vector.quantize_mx(out=x_codes[0][:].bitcast(FP8X4), scales=x_sc[0][:], in_=x0[:])
                last_banks = [psum.tile([P, 2, PIECE], F32, name="h_bank") for half in range(2)]
                score_pass(0, last_banks, PIECES - 1)
            else:
                finish_scores(k - 1)
            nc.vector.tensor_tensor(
                halves[k][:, 1, :].bitcast(BF16).rearrange("p (m e) -> p m e", e=2),
                last[:].rearrange("p e m -> p m e"),
                loaded[1][1][:, :, cols(k)].rearrange("p e m -> p m e"),
                ADD,
            )
            x = keep.tile([P, PIECE * PACK], BF16, name="x1_%d" % k, align_bytes=64)
            weave(x[:], halves[k][:])
            x1.append(x)
        store(1)
        finish_scores(PIECES - 1)
        for k in range(2, PIECES):
            store(k)
